import numpy as np
import ml_dtypes


def mxq(x, axis, fmt="e4m3"):
    dtype, down = {"e4m3": (ml_dtypes.float8_e4m3fn, 7), "e5m2": (ml_dtypes.float8_e5m2, 14)}[fmt]
    v = np.moveaxis(np.asarray(x, np.float32).astype(ml_dtypes.bfloat16).astype(np.float64), axis, -1)
    blocks = v.reshape(v.shape[:-1] + (-1, 32))
    amax = np.abs(blocks).max(-1, keepdims=True)
    byte = np.maximum(np.where(amax > 0, np.frexp(amax)[1] - 1 + 127, 0) - down, 1)
    scale = np.exp2(byte - 127.0)
    codes = (blocks / scale).astype(np.float32).astype(dtype).astype(np.float64)
    return np.moveaxis((codes * scale).reshape(v.shape), -1, axis)


WIDE = False


def mx_kscale(k):
    if not WIDE:
        return np.ones(k)
    levels = np.array([10, -10, 5, -5, 0])
    if k % 512:
        return np.exp2(np.random.permutation(np.resize(levels, k // 32))).repeat(32)
    a = np.empty((k // 512, 16))
    for p in range(k // 512):
        a[p, :8] = np.random.permutation(np.resize(levels, 8))
        for g in range(8):
            far = levels[np.abs(levels - a[p, g]) >= 10]
            a[p, g + 8] = far[np.random.randint(len(far))]
    return np.exp2(a.ravel()).repeat(32)


def f64(x):
    return np.asarray(x).astype(np.float64)


def striped(idx):
    return np.tile(idx.reshape(-1, 16).T, (8, 1)).astype(np.uint16)


def unstriped(offs):
    return offs[:16].T.reshape(-1).astype(np.int64)


def striped8(idx):
    return np.concatenate([x.reshape(-1, 16).T for x in idx]).astype(np.uint16)


def runs(offs, k):
    lists = np.stack([offs[16 * r : 16 * r + 16].T.reshape(-1) for r in range(8)]).astype(np.int64)
    return lists[np.arange(k) % 512 // 64]


def pack_weight(w):
    k, n = w.shape
    w = f64(np.asarray(w, np.float32).astype(ml_dtypes.bfloat16)).reshape(k // 32, 32, n)
    amax = np.abs(w).max(1)
    byte = np.clip(np.where(amax > 0, np.frexp(amax)[1] - 1 + 127 - 7, 1), 1, 254)
    scaled = (w * np.exp2(127.0 - byte)[:, None, :]).reshape(k, n).astype(np.float32)
    words = np.ascontiguousarray(scaled.reshape(k // 512, 128, 4, n).transpose(0, 1, 3, 2)).astype(ml_dtypes.float8_e4m3fn).view(np.uint8)
    return words, np.ascontiguousarray(byte.astype(np.uint8).reshape(k // 512, 16, n))


def unpack_weight(words, scales):
    g, p, n, _ = words.shape
    vals = np.ascontiguousarray(words).view(ml_dtypes.float8_e4m3fn).astype(np.float64) * np.repeat(np.exp2(scales.astype(np.float64) - 127.0), 8, axis=1)[..., None]
    return vals.transpose(0, 1, 3, 2).reshape(g * 512, n)


E2M1 = np.array([0.0, 0.5, 1.0, 1.5, 2.0, 3.0, 4.0, 6.0, -0.0, -0.5, -1.0, -1.5, -2.0, -3.0, -4.0, -6.0])


def pack_fp4(w):
    k, n = w.shape
    w = f64(np.asarray(w, np.float32).astype(ml_dtypes.bfloat16)).reshape(k // 32, 32, n)
    amax = np.abs(w).max(1)
    mant, ex = np.frexp(amax / 6.0)
    byte = np.clip(np.where(amax > 0, np.where(mant > 0.5, ex, ex - 1) + 127, 1), 1, 254)
    scaled = (w * np.exp2(127.0 - byte)[:, None, :]).reshape(k, n).astype(np.float32)
    c = np.ascontiguousarray(scaled.reshape(k // 512, 128, 4, n).transpose(0, 1, 3, 2)).astype(ml_dtypes.float4_e2m1fn).view(np.uint8) & 0xF
    words = (c[..., 0::2] | (c[..., 1::2] << 4)).reshape(k // 512, 128, 2 * n)
    return np.ascontiguousarray(words), np.ascontiguousarray(byte.astype(np.uint8).reshape(k // 512, 16, n))


def unpack_fp4(words, scales):
    g, _, n = scales.shape
    words = np.ascontiguousarray(words).reshape(g, 128, n, 2)
    nib = np.empty((g, 128, n, 4), np.uint8)
    nib[..., 0::2] = words & 0xF
    nib[..., 1::2] = words >> 4
    vals = E2M1[nib] * np.repeat(np.exp2(scales.astype(np.float64) - 127.0), 8, axis=1)[..., None]
    return vals.transpose(0, 1, 3, 2).reshape(g * 512, n)


def sigmoid(v):
    return 1.0 / (1.0 + np.exp(-np.maximum(v, -700.0)))

def planes(y):
    n, m = y.shape
    v = y.astype(np.float32).astype(ml_dtypes.bfloat16).astype(np.float64).reshape(n // 32, 32, m)
    top = np.abs(v).max(1)
    byte = np.clip(np.where(top > 0, np.frexp(top)[1] - 1 + 127 - 7, 1), 1, 254)
    codes = (v * np.exp2(127.0 - byte)[:, None, :]).reshape(n, m).astype(np.float32).astype(ml_dtypes.float8_e4m3fn).view(np.uint8)
    words = codes.reshape(n // 512, 128, 4, m).transpose(0, 1, 3, 2)
    return np.ascontiguousarray(words), np.ascontiguousarray(byte.astype(np.uint8).reshape(n // 512, 16, m))


K, T, S, H, C, U = 512, 2048, 512, 512, 512, 1024


def setup_inputs():
    n = np.random.standard_normal
    s = mx_kscale(K)[:, None]
    packed_xT = pack_weight(n((K, T)) * s)
    packed_w1 = pack_fp4(n((K, H)) / np.sqrt(K) / s)
    packed_w2 = pack_fp4(n((K, H)) / np.sqrt(K) / s)
    return {
        "x_words": packed_xT[0],
        "x_scales": packed_xT[1],
        "w1_words": packed_w1[0],
        "w1_scales": packed_w1[1],
        "w2_words": packed_w2[0],
        "w2_scales": packed_w2[1],
        "gs": (np.random.uniform(0.5, 1.5, (K, 1)) / s).astype(np.float32),
        "mem": n((C, U)).astype(np.float32),
        "offs": striped(np.random.permutation(T)[:S]),
        "two": striped(np.random.permutation(T)[:S]),
        "n1": striped8(np.stack([np.random.permutation(S) for _ in range(8)])),
        "n2": striped8(np.stack([np.random.permutation(S) for _ in range(8)])),
        "cand": striped(np.random.permutation(T)[:C]),
        "n3": striped8(np.stack([np.random.permutation(U)[:S] for _ in range(8)])),
    }


def reference(x_words, x_scales, w1_words, w1_scales, w2_words, w2_scales, gs, mem, offs, two, n1, n2, cand, n3):
    x_cand = unpack_weight(x_words, x_scales)[:, unstriped(cand)]
    xq = unpack_weight(x_words, x_scales)[:, unstriped(offs)]
    y = unpack_fp4(w1_words, w1_scales).T @ xq
    x_two = unpack_weight(x_words, x_scales)[:, unstriped(two)]
    d = unpack_fp4(w2_words, w2_scales).T @ x_two
    z = f64(gs) * ((y + y[np.arange(H)[:, None], runs(n1, H)]) * (sigmoid(d + d[np.arange(H)[:, None], runs(n2, H)])))
    s = 0.0625 * ((x_cand.T @ mxq(z, 0, "e4m3")))
    out = f64(mem).copy()
    out[np.arange(C)[:, None], runs(n3, C)] = s
    return (out,) + planes(out)

@@ -1,0 +1,220 @@
+from contextlib import ExitStack
+
+import concourse.mybir as mybir
+
+F32 = mybir.dt.float32
+BF16 = mybir.dt.bfloat16
+I32 = mybir.dt.int32
+U32 = mybir.dt.uint32
+U16 = mybir.dt.uint16
+U8 = mybir.dt.uint8
+FP8X4 = mybir.dt.float8_e4m3fn_x4
+FP4X4 = mybir.dt.float4_e2m1fn_x4
+ACT = mybir.ActivationFunctionType
+ALU = mybir.AluOpType
+
+P = 128
+PACK = 4
+T = 2048
+S = 512
+U = 1024
+HALF = S // 2
+FLOPS = 3 * 2 * 512 * 512 * 512
+
+
+def load_scale_rows(queue, plane, rows):
+    for q in range(4):
+        queue.dma_start(out=plane[32 * q : 32 * q + 4, :].bitcast(I32), in_=rows[0, 4 * q : 4 * q + 4, :].bitcast(I32))
+
+
+def tile_picked_twctriebpage_none_po_kernel(
+    tc, x_words, x_scales, w1_words, w1_scales, w2_words, w2_scales, gs, mem, offs, two, n1, n2, cand, n3, out_0, out_1, out_2
+):
+    nc = tc.nc
+    with ExitStack() as ctx:
+        lists = ctx.enter_context(tc.tile_pool(name="lists", bufs=1))
+        sb = ctx.enter_context(tc.tile_pool(name="sb", bufs=1))
+        psum = ctx.enter_context(tc.psum_pool(name="psum", bufs=1))
+
+        def new(shape, dtype, name, tag=None):
+            return sb.tile(shape, dtype, name=name, tag=tag or name, align_bytes=64)
+
+        def load_list(src, name):
+            tile = lists.tile([P, S // 16], U16, name=name)
+            nc.sync.dma_start(tile[:], src)
+            return tile
+
+        x_sc = new([P, T], U8, "x_sc")
+        nc.vector.memset(x_sc[:].bitcast(I32), 0)
+        w2_sc = new([P, S], U8, "w2_sc")
+        nc.vector.memset(w2_sc[:].bitcast(I32), 0)
+        w1_sc = new([P, S], U8, "w1_sc")
+        nc.vector.memset(w1_sc[:].bitcast(I32), 0)
+
+        load_scale_rows(nc.sync, x_sc, x_scales)
+        two_l = load_list(two, "two_l")
+        offs_l = load_list(offs, "offs_l")
+        w2_raw = new([P, 2 * S], U8, "w2_raw")
+        nc.sync.dma_start(out=w2_raw[:].bitcast(I32), in_=w2_words[0].bitcast(I32))
+        cand_l = load_list(cand, "cand_l")
+        x_w = new([P, T], I32, "x_w")
+        nc.sync.dma_start(out=x_w[:], in_=x_words[0].rearrange("p c r -> p (c r)").bitcast(I32))
+        load_scale_rows(nc.sync, w2_sc, w2_scales)
+        w1_raw = new([P, 2 * S], U8, "w1_raw")
+        nc.sync.dma_start(out=w1_raw[:].bitcast(I32), in_=w1_words[0].bitcast(I32))
+        load_scale_rows(nc.sync, w1_sc, w1_scales)
+        gs_t = new([P, PACK], F32, "gs_t")
+        nc.sync.dma_start(out=gs_t[:], in_=gs.rearrange("(p t) o -> p (t o)", t=PACK))
+        n2_l = load_list(n2, "n2_l")
+        n1_l = load_list(n1, "n1_l")
+        n3_l = load_list(n3, "n3_l")
+        mem_v = mem.rearrange("(p t) u -> t p u", t=PACK)
+        out_v = out_0.rearrange("(p t) u -> t p u", t=PACK)
+        order = (2, 0, 1, 3)
+        page = {}
+        for t in order:
+            page[t] = new([P, U], F32, "page%d" % t)
+            nc.sync.dma_start(out=page[t][:], in_=mem_v[t])
+
+        half_gs = new([P, PACK], F32, "half_gs")
+        nc.scalar.activation(half_gs[:], gs_t[:], ACT.Copy, scale=0.5)
+
+        def gather_bytes(lst, name, tag=None):
+            tile = new([P, S], U8, name, tag)
+            nc.vector.tensor_copy(tile[:], x_sc[:].indirect(lst[:]))
+            return tile
+
+        def gather_words(lst, name, tag=None):
+            tile = new([P, S], U32, name, tag)
+            nc.vector.tensor_copy(tile[:], x_w[:].bitcast(U32).indirect(lst[:]))
+            return tile
+
+        def deal(src, width, dtype, name, tag=None):
+            tile = new([P, S * width], dtype, name, tag)
+            nc.vector.tensor_copy(
+                tile[:].rearrange("p (t m b) -> p t m b", t=PACK, b=width),
+                src.rearrange("p (m t b) -> p t m b", t=PACK, b=width),
+            )
+            return tile
+
+        two_sc = gather_bytes(two_l, "two_sc")
+        offs_sc = gather_bytes(offs_l, "offs_sc")
+        w2_d = deal(w2_raw[:], 2, U8, "w2_d")
+        w2_sc_d = deal(w2_sc[:], 1, U8, "w2_sc_d")
+        two_w = gather_words(two_l, "two_w")
+        offs_w = gather_words(offs_l, "offs_w")
+        w1_d = deal(w1_raw[:], 2, U8, "w1_d")
+        w1_sc_d = deal(w1_sc[:], 1, U8, "w1_sc_d")
+        cand_sc = gather_bytes(cand_l, "cand_sc")
+
+        def project(w_d, w_sc_d, words, scales, t, bank):
+            acc = psum.tile([P, S], F32, name="bank%d" % bank, tag="bank%d" % bank)
+            nc.tensor.matmul_mx(
+                out=acc[:],
+                lhsT=w_d[:, 2 * P * t : 2 * P * (t + 1)].bitcast(FP4X4),
+                lhsT_scale=w_sc_d[:, P * t : P * (t + 1)],
+                rhs=words[:].bitcast(FP8X4),
+                rhs_scale=scales[:],
+                start=True,
+                stop=True,
+            )
+            return acc
+
+        d_acc = [project(w2_d, w2_sc_d, two_w, two_sc, t, t) for t in range(PACK)]
+        y_acc = [project(w1_d, w1_sc_d, offs_w, offs_sc, t, PACK + t) for t in range(PACK)]
+
+        win = [new([P, S], F32, "win0")] + [new([P, 2 * S], F32, "win%d" % i) for i in range(1, 2 * PACK)]
+        last_copy = new([P, S], F32, "last_copy")
+
+        def plain(i):
+            return win[i + 1][:, S:] if i + 1 < 2 * PACK else last_copy[:]
+
+        def pair_sum(i, lst, name):
+            total = new([P, S], F32, name)
+            if i == 0:
+                for h in range(2):
+                    cols = slice(h * HALF, (h + 1) * HALF)
+                    nc.vector.tensor_tensor(
+                        total[:, cols], win[0][:].indirect(lst[:, h * 16 : (h + 1) * 16]), plain(0)[:, cols], ALU.add
+                    )
+            else:
+                nc.vector.tensor_tensor(total[:], win[i][:].indirect(lst[:]), plain(i), ALU.add)
+            return total
+
+        d_sum = []
+        for t in range(PACK):
+            nc.scalar.copy(win[t][:, :S], d_acc[t][:])
+            nc.scalar.copy(plain(t), d_acc[t][:])
+            d_sum.append(pair_sum(t, n2_l, "d_sum%d" % t))
+
+        z_rows = new([P, PACK, S], BF16, "z_rows")
+        th = []
+        y_sum = []
+
+        def gate(t):
+            nc.vector.scalar_tensor_tensor(z_rows[:, t, :], th[t][:], 1.0, y_sum[t][:], ALU.add, ALU.mult)
+
+        for t in range(PACK):
+            i = PACK + t
+            nc.scalar.activation(win[i][:, :S], y_acc[t][:], ACT.Copy, scale=half_gs[:, t : t + 1])
+            nc.scalar.activation(plain(i), y_acc[t][:], ACT.Copy, scale=half_gs[:, t : t + 1])
+            th.append(new([P, S], F32, "th%d" % t))
+            nc.scalar.activation(th[t][:], d_sum[t][:], ACT.Tanh, scale=0.5)
+            y_sum.append(pair_sum(i, n1_l, "y_sum%d" % t))
+            if t > 0:
+                gate(t - 1)
+        gate(PACK - 1)
+
+        cand_w = gather_words(cand_l, "cand_w", tag="win7")
+        cand_sc_d = deal(cand_sc[:], 1, U8, "cand_sc_d", tag="last_copy")
+        cand_w_d = deal(cand_w[:].bitcast(I32), 1, I32, "cand_w_d")
+
+        z_in = new([P, S * PACK], BF16, "z_in")
+        z_w = new([P, S], U32, "z_w")
+        z_sc = new([P, S], U8, "z_sc")
+        for h in range(2):
+            cols = slice(h * HALF, (h + 1) * HALF)
+            wide = slice(PACK * h * HALF, PACK * (h + 1) * HALF)
+            nc.scalar.copy(
+                z_in[:, wide].rearrange("p (c i t) -> p c t i", i=4, t=PACK),
+                z_rows[:, :, cols].rearrange("p t (c i) -> p c t i", i=4),
+            )
+            nc.vector.quantize_mx(out=z_w[:, cols].bitcast(FP8X4), scales=z_sc[:, cols], in_=z_in[:, wide])
+
+        out_in = new([P, U, PACK], BF16, "out_in")
+        for n, t in enumerate(order):
+            acc = psum.tile([P, S], F32, name="score%d" % n, tag="bank%d" % n)
+            score = new([P, S], F32, "score_sb%d" % n)
+            pieces = (slice(0, HALF), slice(HALF, S)) if n == 0 else (slice(0, S),)
+            for cols in pieces:
+                nc.tensor.matmul_mx(
+                    out=acc[:, cols],
+                    lhsT=cand_w_d[:, P * t : P * (t + 1)].bitcast(FP8X4),
+                    lhsT_scale=cand_sc_d[:, P * t : P * (t + 1)],
+                    rhs=z_w[:, cols].bitcast(FP8X4),
+                    rhs_scale=z_sc[:, cols],
+                    start=True,
+                    stop=True,
+                )
+                nc.scalar.activation(score[:, cols], acc[:, cols], ACT.Copy, scale=0.0625)
+                nc.vector.tensor_copy(page[t][:].indirect(n3_l[:, cols.start // 16 : cols.stop // 16]), score[:, cols])
+            nc.sync.dma_start(out=out_v[t], in_=page[t][:])
+            if n < PACK - 1:
+                nc.scalar.copy(out_in[:, :, t], page[t][:])
+            else:
+                nc.vector.tensor_copy(out_in[:, : U // 2, t], page[t][:, : U // 2])
+                nc.scalar.copy(out_in[:, U // 2 :, t], page[t][:, U // 2 :])
+
+        out_w = new([P, U], U32, "out_w")
+        out_sc = new([P, U], U8, "out_sc")
+        words_v = out_1[0].rearrange("p c r -> p (c r)").bitcast(I32)
+        for h in range(2):
+            cols = slice(h * U // 2, (h + 1) * U // 2)
+            nc.vector.quantize_mx(
+                out=out_w[:, cols].bitcast(FP8X4),
+                scales=out_sc[:, cols],
+                in_=out_in[:, cols, :].rearrange("p c t -> p (c t)"),
+            )
+            nc.sync.dma_start(out=words_v[:, cols], in_=out_w[:, cols].bitcast(I32))
+        for q in range(4):
+            nc.scalar.dma_start(out=out_2[0, 4 * q : 4 * q + 4, :].bitcast(I32), in_=out_sc[32 * q : 32 * q + 4, :].bitcast(I32))

@@ -51,26 +51,26 @@ def tile_picked_twctriebpage_none_po_kernel(
         w1_sc = new([P, S], U8, "w1_sc")
         nc.vector.memset(w1_sc[:].bitcast(I32), 0)
 
-        load_scale_rows(nc.sync, x_sc, x_scales)
-        two_l = load_list(two, "two_l")
-        offs_l = load_list(offs, "offs_l")
         w2_raw = new([P, 2 * S], U8, "w2_raw")
         nc.sync.dma_start(out=w2_raw[:].bitcast(I32), in_=w2_words[0].bitcast(I32))
-        cand_l = load_list(cand, "cand_l")
+        w1_raw = new([P, 2 * S], U8, "w1_raw")
+        nc.sync.dma_start(out=w1_raw[:].bitcast(I32), in_=w1_words[0].bitcast(I32))
+        load_scale_rows(nc.sync, x_sc, x_scales)
+        two_l = load_list(two, "two_l")
         x_w = new([P, T], I32, "x_w")
         nc.sync.dma_start(out=x_w[:], in_=x_words[0].rearrange("p c r -> p (c r)").bitcast(I32))
         load_scale_rows(nc.sync, w2_sc, w2_scales)
-        w1_raw = new([P, 2 * S], U8, "w1_raw")
-        nc.sync.dma_start(out=w1_raw[:].bitcast(I32), in_=w1_words[0].bitcast(I32))
+        offs_l = load_list(offs, "offs_l")
         load_scale_rows(nc.sync, w1_sc, w1_scales)
         gs_t = new([P, PACK], F32, "gs_t")
         nc.sync.dma_start(out=gs_t[:], in_=gs.rearrange("(p t) o -> p (t o)", t=PACK))
         n2_l = load_list(n2, "n2_l")
         n1_l = load_list(n1, "n1_l")
+        cand_l = load_list(cand, "cand_l")
         n3_l = load_list(n3, "n3_l")
         mem_v = mem.rearrange("(p t) u -> t p u", t=PACK)
         out_v = out_0.rearrange("(p t) u -> t p u", t=PACK)
-        order = (2, 0, 1, 3)
+        order = (0, 2, 3, 1)
         page = {}
         for t in order:
             page[t] = new([P, U], F32, "page%d" % t)
@@ -89,23 +89,13 @@ def tile_picked_twctriebpage_none_po_kernel(
             nc.vector.tensor_copy(tile[:], x_w[:].bitcast(U32).indirect(lst[:]))
             return tile
 
-        def deal(src, width, dtype, name, tag=None):
-            tile = new([P, S * width], dtype, name, tag)
+        def deal(src, width, dtype, name, tag=None, lo=0, hi=PACK):
+            tile = new([P, P * (hi - lo) * width], dtype, name, tag)
             nc.vector.tensor_copy(
-                tile[:].rearrange("p (t m b) -> p t m b", t=PACK, b=width),
-                src.rearrange("p (m t b) -> p t m b", t=PACK, b=width),
+                tile[:].rearrange("p (t m b) -> p t m b", t=hi - lo, b=width),
+                src.rearrange("p (m t b) -> p t m b", t=PACK, b=width)[:, lo:hi],
             )
             return tile
-
-        two_sc = gather_bytes(two_l, "two_sc")
-        offs_sc = gather_bytes(offs_l, "offs_sc")
-        w2_d = deal(w2_raw[:], 2, U8, "w2_d")
-        w2_sc_d = deal(w2_sc[:], 1, U8, "w2_sc_d")
-        two_w = gather_words(two_l, "two_w")
-        offs_w = gather_words(offs_l, "offs_w")
-        w1_d = deal(w1_raw[:], 2, U8, "w1_d")
-        w1_sc_d = deal(w1_sc[:], 1, U8, "w1_sc_d")
-        cand_sc = gather_bytes(cand_l, "cand_sc")
 
         def project(w_d, w_sc_d, words, scales, t, bank):
             acc = psum.tile([P, S], F32, name="bank%d" % bank, tag="bank%d" % bank)
@@ -120,7 +110,16 @@ def tile_picked_twctriebpage_none_po_kernel(
             )
             return acc
 
+        w2_d = deal(w2_raw[:], 2, U8, "w2_d")
+        two_sc = gather_bytes(two_l, "two_sc")
+        two_w = gather_words(two_l, "two_w")
+        w2_sc_d = deal(w2_sc[:], 1, U8, "w2_sc_d")
         d_acc = [project(w2_d, w2_sc_d, two_w, two_sc, t, t) for t in range(PACK)]
+        offs_w = gather_words(offs_l, "offs_w")
+        offs_sc = gather_bytes(offs_l, "offs_sc")
+        w1_d = deal(w1_raw[:], 2, U8, "w1_d")
+        w1_sc_d = deal(w1_sc[:], 1, U8, "w1_sc_d")
+
         y_acc = [project(w1_d, w1_sc_d, offs_w, offs_sc, t, PACK + t) for t in range(PACK)]
 
         win = [new([P, S], F32, "win0")] + [new([P, 2 * S], F32, "win%d" % i) for i in range(1, 2 * PACK)]
@@ -152,58 +151,77 @@ def tile_picked_twctriebpage_none_po_kernel(
         y_sum = []
 
         def gate(t):
+            th.append(new([P, S], F32, "th%d" % t))
+            nc.scalar.activation(th[t][:], d_sum[t][:], ACT.Tanh, scale=0.5)
             nc.vector.scalar_tensor_tensor(z_rows[:, t, :], th[t][:], 1.0, y_sum[t][:], ALU.add, ALU.mult)
 
         for t in range(PACK):
             i = PACK + t
             nc.scalar.activation(win[i][:, :S], y_acc[t][:], ACT.Copy, scale=half_gs[:, t : t + 1])
             nc.scalar.activation(plain(i), y_acc[t][:], ACT.Copy, scale=half_gs[:, t : t + 1])
-            th.append(new([P, S], F32, "th%d" % t))
-            nc.scalar.activation(th[t][:], d_sum[t][:], ACT.Tanh, scale=0.5)
             y_sum.append(pair_sum(i, n1_l, "y_sum%d" % t))
             if t > 0:
                 gate(t - 1)
         gate(PACK - 1)
 
-        cand_w = gather_words(cand_l, "cand_w", tag="win7")
-        cand_sc_d = deal(cand_sc[:], 1, U8, "cand_sc_d", tag="last_copy")
-        cand_w_d = deal(cand_w[:].bitcast(I32), 1, I32, "cand_w_d")
+        cand_w = gather_words(cand_l, "cand_w", tag="y_sum3")
+        cand_sc = gather_bytes(cand_l, "cand_sc", tag="th3")
+        first_w = deal(cand_w[:].bitcast(I32), 1, I32, "first_w", hi=1)
+        first_sc = deal(cand_sc[:], 1, U8, "first_sc", hi=1)
 
-        z_in = new([P, S * PACK], BF16, "z_in")
         z_w = new([P, S], U32, "z_w")
         z_sc = new([P, S], U8, "z_sc")
         for h in range(2):
             cols = slice(h * HALF, (h + 1) * HALF)
-            wide = slice(PACK * h * HALF, PACK * (h + 1) * HALF)
+            z_in = new([P, HALF * PACK], BF16, "z_in%d" % h)
             nc.scalar.copy(
-                z_in[:, wide].rearrange("p (c i t) -> p c t i", i=4, t=PACK),
+                z_in[:].rearrange("p (c i t) -> p c t i", i=4, t=PACK),
                 z_rows[:, :, cols].rearrange("p t (c i) -> p c t i", i=4),
             )
-            nc.vector.quantize_mx(out=z_w[:, cols].bitcast(FP8X4), scales=z_sc[:, cols], in_=z_in[:, wide])
+            nc.vector.quantize_mx(out=z_w[:, cols].bitcast(FP8X4), scales=z_sc[:, cols], in_=z_in[:])
+        rest_w = deal(cand_w[:].bitcast(I32), 1, I32, "rest_w", tag="z_in0", lo=1)
+        rest_sc = deal(cand_sc[:], 1, U8, "rest_sc", tag="z_in1", lo=1)
 
         out_in = new([P, U, PACK], BF16, "out_in")
-        for n, t in enumerate(order):
+        SPLIT = 768
+
+        def score_rows(n):
+            t = order[n]
             acc = psum.tile([P, S], F32, name="score%d" % n, tag="bank%d" % n)
-            score = new([P, S], F32, "score_sb%d" % n)
+            score = new([P, S], F32, "score_sb%d" % n, tag="score_sb0" if n == PACK - 1 else None)
+            cw = first_w[:] if t == 0 else rest_w[:, P * (t - 1) : P * t]
+            cs = first_sc[:] if t == 0 else rest_sc[:, P * (t - 1) : P * t]
             pieces = (slice(0, HALF), slice(HALF, S)) if n == 0 else (slice(0, S),)
             for cols in pieces:
                 nc.tensor.matmul_mx(
                     out=acc[:, cols],
-                    lhsT=cand_w_d[:, P * t : P * (t + 1)].bitcast(FP8X4),
-                    lhsT_scale=cand_sc_d[:, P * t : P * (t + 1)],
+                    lhsT=cw.bitcast(FP8X4),
+                    lhsT_scale=cs,
                     rhs=z_w[:, cols].bitcast(FP8X4),
                     rhs_scale=z_sc[:, cols],
                     start=True,
                     stop=True,
                 )
                 nc.scalar.activation(score[:, cols], acc[:, cols], ACT.Copy, scale=0.0625)
+            return score, pieces
+
+        def write_page(n, score, pieces):
+            t = order[n]
+            for cols in pieces:
                 nc.vector.tensor_copy(page[t][:].indirect(n3_l[:, cols.start // 16 : cols.stop // 16]), score[:, cols])
             nc.sync.dma_start(out=out_v[t], in_=page[t][:])
             if n < PACK - 1:
                 nc.scalar.copy(out_in[:, :, t], page[t][:])
             else:
                 nc.vector.tensor_copy(out_in[:, : U // 2, t], page[t][:, : U // 2])
-                nc.scalar.copy(out_in[:, U // 2 :, t], page[t][:, U // 2 :])
+                nc.vector.tensor_copy(out_in[:, U // 2 : SPLIT, t], page[t][:, U // 2 : SPLIT])
+                nc.scalar.copy(out_in[:, SPLIT:, t], page[t][:, SPLIT:])
+
+        scores = [score_rows(n) for n in range(PACK - 1)]
+        write_page(0, *scores[0])
+        scores.append(score_rows(PACK - 1))
+        for n in range(1, PACK):
+            write_page(n, *scores[n])
 
         out_w = new([P, U], U32, "out_w")
         out_sc = new([P, U], U8, "out_sc")

@@ -53,14 +53,14 @@ def tile_picked_twctriebpage_none_po_kernel(
 
         w2_raw = new([P, 2 * S], U8, "w2_raw")
         nc.sync.dma_start(out=w2_raw[:].bitcast(I32), in_=w2_words[0].bitcast(I32))
-        w1_raw = new([P, 2 * S], U8, "w1_raw")
-        nc.sync.dma_start(out=w1_raw[:].bitcast(I32), in_=w1_words[0].bitcast(I32))
         load_scale_rows(nc.sync, x_sc, x_scales)
         two_l = load_list(two, "two_l")
+        offs_l = load_list(offs, "offs_l")
         x_w = new([P, T], I32, "x_w")
         nc.sync.dma_start(out=x_w[:], in_=x_words[0].rearrange("p c r -> p (c r)").bitcast(I32))
         load_scale_rows(nc.sync, w2_sc, w2_scales)
-        offs_l = load_list(offs, "offs_l")
+        w1_raw = new([P, 2 * S], U8, "w1_raw")
+        nc.sync.dma_start(out=w1_raw[:].bitcast(I32), in_=w1_words[0].bitcast(I32))
         load_scale_rows(nc.sync, w1_sc, w1_scales)
         gs_t = new([P, PACK], F32, "gs_t")
         nc.sync.dma_start(out=gs_t[:], in_=gs.rearrange("(p t) o -> p (t o)", t=PACK))
@@ -115,7 +115,7 @@ def tile_picked_twctriebpage_none_po_kernel(
         two_w = gather_words(two_l, "two_w")
         w2_sc_d = deal(w2_sc[:], 1, U8, "w2_sc_d")
         d_acc = [project(w2_d, w2_sc_d, two_w, two_sc, t, t) for t in range(PACK)]
-        offs_w = gather_words(offs_l, "offs_w")
+        offs_w = gather_words(offs_l, "offs_w", tag="w2_sc")
         offs_sc = gather_bytes(offs_l, "offs_sc")
         w1_d = deal(w1_raw[:], 2, U8, "w1_d")
         w1_sc_d = deal(w1_sc[:], 1, U8, "w1_sc_d")

from contextlib import ExitStack

import concourse.mybir as mybir

F32 = mybir.dt.float32
BF16 = mybir.dt.bfloat16
I32 = mybir.dt.int32
U32 = mybir.dt.uint32
U16 = mybir.dt.uint16
U8 = mybir.dt.uint8
FP8X4 = mybir.dt.float8_e4m3fn_x4
FP4X4 = mybir.dt.float4_e2m1fn_x4
ACT = mybir.ActivationFunctionType
ALU = mybir.AluOpType

P = 128
PACK = 4
T = 2048
S = 512
U = 1024
HALF = S // 2
FLOPS = 3 * 2 * 512 * 512 * 512


def load_scale_rows(queue, plane, rows):
    for q in range(4):
        queue.dma_start(out=plane[32 * q : 32 * q + 4, :].bitcast(I32), in_=rows[0, 4 * q : 4 * q + 4, :].bitcast(I32))


def tile_picked_twctriebpage_none_po_kernel(
    tc, x_words, x_scales, w1_words, w1_scales, w2_words, w2_scales, gs, mem, offs, two, n1, n2, cand, n3, out_0, out_1, out_2
):
    nc = tc.nc
    with ExitStack() as ctx:
        lists = ctx.enter_context(tc.tile_pool(name="lists", bufs=1))
        sb = ctx.enter_context(tc.tile_pool(name="sb", bufs=1))
        psum = ctx.enter_context(tc.psum_pool(name="psum", bufs=1))

        def new(shape, dtype, name, tag=None):
            return sb.tile(shape, dtype, name=name, tag=tag or name, align_bytes=64)

        def load_list(src, name):
            tile = lists.tile([P, S // 16], U16, name=name)
            nc.sync.dma_start(tile[:], src)
            return tile

        x_sc = new([P, T], U8, "x_sc")
        nc.vector.memset(x_sc[:].bitcast(I32), 0)
        w2_sc = new([P, S], U8, "w2_sc")
        nc.vector.memset(w2_sc[:].bitcast(I32), 0)
        w1_sc = new([P, S], U8, "w1_sc")
        nc.vector.memset(w1_sc[:].bitcast(I32), 0)

        w2_raw = new([P, 2 * S], U8, "w2_raw")
        nc.sync.dma_start(out=w2_raw[:].bitcast(I32), in_=w2_words[0].bitcast(I32))
        load_scale_rows(nc.sync, x_sc, x_scales)
        two_l = load_list(two, "two_l")
        offs_l = load_list(offs, "offs_l")
        x_w = new([P, T], I32, "x_w")
        nc.sync.dma_start(out=x_w[:], in_=x_words[0].rearrange("p c r -> p (c r)").bitcast(I32))
        load_scale_rows(nc.sync, w2_sc, w2_scales)
        w1_raw = new([P, 2 * S], U8, "w1_raw")
        nc.sync.dma_start(out=w1_raw[:].bitcast(I32), in_=w1_words[0].bitcast(I32))
        load_scale_rows(nc.sync, w1_sc, w1_scales)
        gs_t = new([P, PACK], F32, "gs_t")
        nc.sync.dma_start(out=gs_t[:], in_=gs.rearrange("(p t) o -> p (t o)", t=PACK))
        n2_l = load_list(n2, "n2_l")
        n1_l = load_list(n1, "n1_l")
        cand_l = load_list(cand, "cand_l")
        n3_l = load_list(n3, "n3_l")
        mem_v = mem.rearrange("(p t) u -> t p u", t=PACK)
        out_v = out_0.rearrange("(p t) u -> t p u", t=PACK)
        order = (0, 2, 3, 1)
        page = {}
        for t in order:
            page[t] = new([P, U], F32, "page%d" % t)
            nc.sync.dma_start(out=page[t][:], in_=mem_v[t])

        half_gs = new([P, PACK], F32, "half_gs")
        nc.scalar.activation(half_gs[:], gs_t[:], ACT.Copy, scale=0.5)

        def gather_bytes(lst, name, tag=None):
            tile = new([P, S], U8, name, tag)
            nc.vector.tensor_copy(tile[:], x_sc[:].indirect(lst[:]))
            return tile

        def gather_words(lst, name, tag=None):
            tile = new([P, S], U32, name, tag)
            nc.vector.tensor_copy(tile[:], x_w[:].bitcast(U32).indirect(lst[:]))
            return tile

        def deal(src, width, dtype, name, tag=None, lo=0, hi=PACK):
            tile = new([P, P * (hi - lo) * width], dtype, name, tag)
            nc.vector.tensor_copy(
                tile[:].rearrange("p (t m b) -> p t m b", t=hi - lo, b=width),
                src.rearrange("p (m t b) -> p t m b", t=PACK, b=width)[:, lo:hi],
            )
            return tile

        def project(w_d, w_sc_d, words, scales, t, bank):
            acc = psum.tile([P, S], F32, name="bank%d" % bank, tag="bank%d" % bank)
            nc.tensor.matmul_mx(
                out=acc[:],
                lhsT=w_d[:, 2 * P * t : 2 * P * (t + 1)].bitcast(FP4X4),
                lhsT_scale=w_sc_d[:, P * t : P * (t + 1)],
                rhs=words[:].bitcast(FP8X4),
                rhs_scale=scales[:],
                start=True,
                stop=True,
            )
            return acc

        w2_d = deal(w2_raw[:], 2, U8, "w2_d")
        two_sc = gather_bytes(two_l, "two_sc")
        two_w = gather_words(two_l, "two_w")
        w2_sc_d = deal(w2_sc[:], 1, U8, "w2_sc_d")
        d_acc = [project(w2_d, w2_sc_d, two_w, two_sc, t, t) for t in range(PACK)]
        offs_w = gather_words(offs_l, "offs_w", tag="w2_sc")
        offs_sc = gather_bytes(offs_l, "offs_sc")
        w1_d = deal(w1_raw[:], 2, U8, "w1_d")
        w1_sc_d = deal(w1_sc[:], 1, U8, "w1_sc_d")

        y_acc = [project(w1_d, w1_sc_d, offs_w, offs_sc, t, PACK + t) for t in range(PACK)]

        win = [new([P, S], F32, "win0")] + [new([P, 2 * S], F32, "win%d" % i) for i in range(1, 2 * PACK)]
        last_copy = new([P, S], F32, "last_copy")

        def plain(i):
            return win[i + 1][:, S:] if i + 1 < 2 * PACK else last_copy[:]

        def pair_sum(i, lst, name):
            total = new([P, S], F32, name)
            if i == 0:
                for h in range(2):
                    cols = slice(h * HALF, (h + 1) * HALF)
                    nc.vector.tensor_tensor(
                        total[:, cols], win[0][:].indirect(lst[:, h * 16 : (h + 1) * 16]), plain(0)[:, cols], ALU.add
                    )
            else:
                nc.vector.tensor_tensor(total[:], win[i][:].indirect(lst[:]), plain(i), ALU.add)
            return total

        d_sum = []
        for t in range(PACK):
            nc.scalar.copy(win[t][:, :S], d_acc[t][:])
            nc.scalar.copy(plain(t), d_acc[t][:])
            d_sum.append(pair_sum(t, n2_l, "d_sum%d" % t))

        z_rows = new([P, PACK, S], BF16, "z_rows")
        th = []
        y_sum = []

        def gate(t):
            th.append(new([P, S], F32, "th%d" % t))
            nc.scalar.activation(th[t][:], d_sum[t][:], ACT.Tanh, scale=0.5)
            nc.vector.scalar_tensor_tensor(z_rows[:, t, :], th[t][:], 1.0, y_sum[t][:], ALU.add, ALU.mult)

        for t in range(PACK):
            i = PACK + t
            nc.scalar.activation(win[i][:, :S], y_acc[t][:], ACT.Copy, scale=half_gs[:, t : t + 1])
            nc.scalar.activation(plain(i), y_acc[t][:], ACT.Copy, scale=half_gs[:, t : t + 1])
            y_sum.append(pair_sum(i, n1_l, "y_sum%d" % t))
            if t > 0:
                gate(t - 1)
        gate(PACK - 1)

        cand_w = gather_words(cand_l, "cand_w", tag="y_sum3")
        cand_sc = gather_bytes(cand_l, "cand_sc", tag="th3")
        first_w = deal(cand_w[:].bitcast(I32), 1, I32, "first_w", hi=1)
        first_sc = deal(cand_sc[:], 1, U8, "first_sc", hi=1)

        z_w = new([P, S], U32, "z_w")
        z_sc = new([P, S], U8, "z_sc")
        for h in range(2):
            cols = slice(h * HALF, (h + 1) * HALF)
            z_in = new([P, HALF * PACK], BF16, "z_in%d" % h)
            nc.scalar.copy(
                z_in[:].rearrange("p (c i t) -> p c t i", i=4, t=PACK),
                z_rows[:, :, cols].rearrange("p t (c i) -> p c t i", i=4),
            )
            nc.vector.quantize_mx(out=z_w[:, cols].bitcast(FP8X4), scales=z_sc[:, cols], in_=z_in[:])
        rest_w = deal(cand_w[:].bitcast(I32), 1, I32, "rest_w", tag="z_in0", lo=1)
        rest_sc = deal(cand_sc[:], 1, U8, "rest_sc", tag="z_in1", lo=1)

        out_in = new([P, U, PACK], BF16, "out_in")
        SPLIT = 768

        def score_rows(n):
            t = order[n]
            acc = psum.tile([P, S], F32, name="score%d" % n, tag="bank%d" % n)
            score = new([P, S], F32, "score_sb%d" % n, tag="score_sb0" if n == PACK - 1 else None)
            cw = first_w[:] if t == 0 else rest_w[:, P * (t - 1) : P * t]
            cs = first_sc[:] if t == 0 else rest_sc[:, P * (t - 1) : P * t]
            pieces = (slice(0, HALF), slice(HALF, S)) if n == 0 else (slice(0, S),)
            for cols in pieces:
                nc.tensor.matmul_mx(
                    out=acc[:, cols],
                    lhsT=cw.bitcast(FP8X4),
                    lhsT_scale=cs,
                    rhs=z_w[:, cols].bitcast(FP8X4),
                    rhs_scale=z_sc[:, cols],
                    start=True,
                    stop=True,
                )
                nc.scalar.activation(score[:, cols], acc[:, cols], ACT.Copy, scale=0.0625)
            return score, pieces

        def write_page(n, score, pieces):
            t = order[n]
            for cols in pieces:
                nc.vector.tensor_copy(page[t][:].indirect(n3_l[:, cols.start // 16 : cols.stop // 16]), score[:, cols])
            nc.sync.dma_start(out=out_v[t], in_=page[t][:])
            if n < PACK - 1:
                nc.scalar.copy(out_in[:, :, t], page[t][:])
            else:
                nc.vector.tensor_copy(out_in[:, : U // 2, t], page[t][:, : U // 2])
                nc.vector.tensor_copy(out_in[:, U // 2 : SPLIT, t], page[t][:, U // 2 : SPLIT])
                nc.scalar.copy(out_in[:, SPLIT:, t], page[t][:, SPLIT:])

        scores = [score_rows(n) for n in range(PACK - 1)]
        write_page(0, *scores[0])
        scores.append(score_rows(PACK - 1))
        for n in range(1, PACK):
            write_page(n, *scores[n])

        out_w = new([P, U], U32, "out_w")
        out_sc = new([P, U], U8, "out_sc")
        words_v = out_1[0].rearrange("p c r -> p (c r)").bitcast(I32)
        for h in range(2):
            cols = slice(h * U // 2, (h + 1) * U // 2)
            nc.vector.quantize_mx(
                out=out_w[:, cols].bitcast(FP8X4),
                scales=out_sc[:, cols],
                in_=out_in[:, cols, :].rearrange("p c t -> p (c t)"),
            )
            nc.sync.dma_start(out=words_v[:, cols], in_=out_w[:, cols].bitcast(I32))
        for q in range(4):
            nc.scalar.dma_start(out=out_2[0, 4 * q : 4 * q + 4, :].bitcast(I32), in_=out_sc[32 * q : 32 * q + 4, :].bitcast(I32))
